import numpy as np
import ml_dtypes


def mxq(x, axis, fmt="e4m3"):
    dtype, down = {"e4m3": (ml_dtypes.float8_e4m3fn, 7), "e5m2": (ml_dtypes.float8_e5m2, 14)}[fmt]
    v = np.moveaxis(np.asarray(x, np.float32).astype(ml_dtypes.bfloat16).astype(np.float64), axis, -1)
    blocks = v.reshape(v.shape[:-1] + (-1, 32))
    amax = np.abs(blocks).max(-1, keepdims=True)
    byte = np.maximum(np.where(amax > 0, np.frexp(amax)[1] - 1 + 127, 0) - down, 1)
    scale = np.exp2(byte - 127.0)
    codes = (blocks / scale).astype(np.float32).astype(dtype).astype(np.float64)
    return np.moveaxis((codes * scale).reshape(v.shape), -1, axis)


WIDE = False


def mx_kscale(k):
    if not WIDE:
        return np.ones(k)
    levels = np.array([10, -10, 5, -5, 0])
    if k % 512:
        return np.exp2(np.random.permutation(np.resize(levels, k // 32))).repeat(32)
    a = np.empty((k // 512, 16))
    for p in range(k // 512):
        a[p, :8] = np.random.permutation(np.resize(levels, 8))
        for g in range(8):
            far = levels[np.abs(levels - a[p, g]) >= 10]
            a[p, g + 8] = far[np.random.randint(len(far))]
    return np.exp2(a.ravel()).repeat(32)


BF16 = ml_dtypes.bfloat16


def bf(x):
    return np.asarray(x, np.float32).astype(BF16)


def f64(x):
    return np.asarray(x).astype(np.float64)


E2M1 = np.array([0.0, 0.5, 1.0, 1.5, 2.0, 3.0, 4.0, 6.0, -0.0, -0.5, -1.0, -1.5, -2.0, -3.0, -4.0, -6.0])


def pack_weight(w, fmt):
    k, n = w.shape
    w = f64(bf(w)).reshape(k // 32, 32, n)
    amax = np.abs(w).max(1)
    if fmt == "e4m3":
        byte = np.frexp(amax)[1] - 1 + 127 - 7
    else:
        mant, ex = np.frexp(amax / 6.0)
        byte = np.where(mant > 0.5, ex, ex - 1) + 127
    byte = np.clip(np.where(amax > 0, byte, 1), 1, 254)
    scaled = (w * np.exp2(127.0 - byte)[:, None, :]).reshape(k, n).astype(np.float32)
    by_word = np.ascontiguousarray(scaled.reshape(k // 512, 128, 4, n).transpose(0, 1, 3, 2))
    if fmt == "e4m3":
        words = by_word.astype(ml_dtypes.float8_e4m3fn).view(np.uint8)
    else:
        c = by_word.astype(ml_dtypes.float4_e2m1fn).view(np.uint8) & 0xF
        words = c[..., 0::2] | (c[..., 1::2] << 4)
    return np.ascontiguousarray(words), np.ascontiguousarray(byte.astype(np.uint8).reshape(k // 512, 16, n))


def unpack_weight(words, scales, fmt):
    g, p, n, _ = words.shape
    if fmt == "e4m3":
        vals = np.ascontiguousarray(words).view(ml_dtypes.float8_e4m3fn).astype(np.float64)
    else:
        nib = np.empty((g, p, n, 4), np.uint8)
        nib[..., 0::2] = words & 0xF
        nib[..., 1::2] = words >> 4
        vals = E2M1[nib]
    vals = vals * np.repeat(np.exp2(scales.astype(np.float64) - 127.0), 8, axis=1)[..., None]
    return vals.transpose(0, 1, 3, 2).reshape(g * 512, n)
def pack4(w):
    words, scales = pack_weight(w, "e2m1")
    return words.reshape(words.shape[0], 128, -1), scales


def unpack4(words, scales):
    return unpack_weight(words.reshape(words.shape[0], 128, -1, 2), scales, "e2m1")


M, K, F = 1024, 512, 1536


def setup_inputs():
    s, t, u = mx_kscale(K), mx_kscale(F), mx_kscale(M)
    x = np.random.standard_normal((M, K)) * s * u[:, None]
    w_in = np.random.standard_normal((K, F)) / np.sqrt(K) / s[:, None] * t
    mix = np.random.standard_normal((M, M)) / np.sqrt(M) / u
    routed = np.random.standard_normal((F, F)) / np.sqrt(F) / t[:, None] * t
    gate = (0.5 + np.random.random(M)) / u
    routed_words, routed_scales = pack4(routed)
    return {"x": bf(x), "w_in": bf(w_in), "mix": bf(mix), "gate": bf(gate),
            "routed_words": routed_words, "routed_scales": routed_scales}


def reference(x, w_in, mix, gate, routed_words, routed_scales):
    h = np.maximum(mxq(f64(x), 1, "e4m3") @ mxq(f64(w_in), 0, "e4m3"), 0.0)
    shared = mxq(f64(mix), 1, "e4m3") @ mxq(h, 0, "e4m3")
    routed = mxq(h, 1, "e4m3") @ unpack4(routed_words, routed_scales)
    return shared + f64(gate)[:, None] * routed

@@ -1,0 +1,295 @@
+from contextlib import ExitStack
+
+import concourse.mybir as mybir
+from concourse.masks import make_identity
+
+M, K, F = 1024, 512, 1536
+FLOPS = 2 * M * K * F + 2 * M * M * F + 2 * M * F * F
+
+F32 = mybir.dt.float32
+BF16 = mybir.dt.bfloat16
+I32 = mybir.dt.int32
+U32 = mybir.dt.uint32
+U8 = mybir.dt.uint8
+FP8X4 = mybir.dt.float8_e4m3fn_x4
+FP4X4 = mybir.dt.float4_e2m1fn_x4
+ACT = mybir.ActivationFunctionType
+ALU = mybir.AluOpType
+
+P = 128
+PACK = 4
+PASS = P * PACK
+GROUPS = M // PASS
+CHUNKS = F // PASS
+BANKS = 8
+HELD = 3
+
+
+def tile_mixer_expert_pair_s8_kernel(tc, x, w_in, mix, gate, routed_words, routed_scales, out):
+    nc = tc.nc
+    with ExitStack() as ctx:
+        keep = ctx.enter_context(tc.tile_pool(name="keep", bufs=1))
+        stage = ctx.enter_context(tc.tile_pool(name="stage", bufs=1))
+        psum = ctx.enter_context(tc.psum_pool(name="psum", bufs=1))
+        ctx.enter_context(tc.manual_schedule())
+
+        x_rows = x.rearrange("(g p t) k -> g p t k", g=GROUPS, t=PACK)
+        mix_rows = mix.rearrange("(g p t) k -> g p t k", g=GROUPS, t=PACK)
+        out_rows = out.rearrange("(g p t) f -> g t p f", g=GROUPS, t=PACK)
+        w_rows = w_in.rearrange("(p j) f -> p j f", j=PACK)
+
+        raw = {}
+        pend = {}
+        codes = {}
+        scales = {}
+        hidden_bf = {}
+        result = {}
+        free = list(range(HELD, BANKS))
+
+        def bank_tile(index):
+            return psum.tile([P, PASS], F32, name="bank%d" % index, tag="bank%d" % index)
+
+        def next_bank():
+            index = free[0]
+            free.remove(index)
+            free.append(index)
+            return bank_tile(index)
+
+        identity = keep.tile([P, P], F32, name="identity")
+        r_scales = keep.tile([P, CHUNKS, F], U8, name="r_scales", align_bytes=64)
+        gate_bf = keep.tile([P, GROUPS, PACK], BF16, name="gate_bf")
+        gate_f32 = keep.tile([P, GROUPS * PACK], F32, name="gate_f32")
+        warm_in = keep.tile([P, 1], F32, name="warm_in")
+        warm_out = keep.tile([P, 1], F32, name="warm_out")
+        nc.vector.memset(warm_in[:], 0.0)
+        nc.scalar.activation(out=warm_out[:], in_=warm_in[:], func=ACT.Relu)
+        make_identity(nc, identity[:])
+        nc.gpsimd.memset(r_scales[:].rearrange("p g n -> p (g n)").bitcast(I32), 0)
+
+        def load_w(c):
+            raw["w", c] = keep.tile([P, PACK, PASS], BF16, name="w_raw%d" % c)
+            nc.sync.dma_start(out=raw["w", c][:], in_=w_rows[:, :, c * PASS : (c + 1) * PASS])
+
+        def load_x(pair):
+            raw["x", pair] = keep.tile([P, 2, K], BF16, name="x_raw%d" % pair)
+            first = 2 * (pair % 2)
+            nc.sync.dma_start(out=raw["x", pair][:], in_=x_rows[pair // 2, :, first : first + 2, :])
+
+        def load_mix(pair):
+            raw["m", pair] = keep.tile([P, 2, M], BF16, name="mix_raw%d" % pair)
+            first = 2 * (pair % 2)
+            nc.sync.dma_start(out=raw["m", pair][:], in_=mix_rows[pair // 2, :, first : first + 2, :])
+
+        def load_r(g):
+            raw["r", g] = keep.tile([P, 2 * F], U8, name="r_words%d" % g, align_bytes=64)
+            nc.sync.dma_start(out=raw["r", g][:].bitcast(I32), in_=routed_words[g].bitcast(I32))
+
+        def load_scales():
+            for q in range(4):
+                nc.sync.dma_start(
+                    out=r_scales[32 * q : 32 * q + 4, :, :].bitcast(I32),
+                    in_=routed_scales[:, 4 * q : 4 * q + 4, :].rearrange("g r n -> r g n").bitcast(I32),
+                )
+
+        def load_gate():
+            nc.sync.dma_start(out=gate_bf[:], in_=gate.rearrange("(g p t) -> p g t", g=GROUPS, t=PACK))
+            nc.gpsimd.tensor_copy(out=gate_f32[:], in_=gate_bf[:].rearrange("p g t -> p (g t)"))
+
+        def copy_on(eng, dst, src):
+            if eng == "V":
+                nc.vector.tensor_copy(out=dst, in_=src)
+            else:
+                nc.scalar.copy(out=dst, in_=src)
+
+        def interleave(key, src, eng, lo, hi):
+            if lo == 0:
+                pend[key] = stage.tile([P, PASS, PACK], BF16, name="wide", tag="wide", bufs=3, align_bytes=64)
+            copy_on(
+                eng,
+                pend[key][:, lo:hi, :].rearrange("p (c i) t -> p c t i", i=4),
+                src[:, :, lo:hi].rearrange("p t (c i) -> p c t i", i=4),
+            )
+
+        def interleave_w(c, eng="V", lo=0, hi=PASS):
+            interleave(("w", c), raw["w", c], eng, lo, hi)
+
+        def interleave_h(g, c, eng="V"):
+            interleave(("h", g, c), hidden_bf[g, c], eng, 0, PASS)
+
+        def quantize(key):
+            src = pend[key]
+            width = src.shape[1]
+            label = "_".join(str(part) for part in key)
+            codes[key] = keep.tile([P, width], U32, name="codes_" + label, align_bytes=64)
+            scales[key] = keep.tile([P, width], U8, name="scales_" + label, align_bytes=64)
+            nc.vector.quantize_mx(
+                out=codes[key][:].bitcast(FP8X4),
+                scales=scales[key][:],
+                in_=src[:].rearrange("p c t -> p (c t)"),
+            )
+
+        def turn(key):
+            bank = next_bank()
+            pend[key] = bank
+            for a in range(2):
+                for u in range(2):
+                    if key[0] == "x":
+                        words = raw[key][:, a, :].bitcast(F32)[:, u : 2 * P : 2]
+                    elif key[0] == "m":
+                        row = raw["m", key[1] // 2][:, key[1] % 2, :].bitcast(F32)
+                        words = row[:, 2 * P * a + u : 2 * P * (a + 1) : 2]
+                    else:
+                        tile_index = 2 * key[1] + a
+                        row = hidden_bf[tile_index // PACK, key[2]][:, tile_index % PACK, :].bitcast(F32)
+                        words = row[:, P * u : P * (u + 1)]
+                    slot = 2 * a + u
+                    nc.tensor.transpose(bank[:, slot * P : (slot + 1) * P], words, identity[:])
+
+        def drain_turn(key, eng="S"):
+            bank = pend[key]
+            pend[key] = stage.tile([P, 2 * P, PACK], BF16, name="turned", tag="turned", bufs=4, align_bytes=64)
+            dst = pend[key][:].rearrange("p c t -> p (c t)").bitcast(F32)
+            copy_on(
+                eng,
+                dst.rearrange("p (a r u) -> p a r u", a=2, u=2),
+                bank[:].rearrange("p (a u r) -> p a r u", a=2, u=2),
+            )
+
+        def hidden(i, c):
+            bank = next_bank()
+            pend["H", i, c] = bank
+            cols = slice(P * (i % 2), P * (i % 2 + 1))
+            nc.tensor.matmul_mx(
+                out=bank[:],
+                lhsT=codes["x", i // 2][:, cols].bitcast(FP8X4),
+                lhsT_scale=scales["x", i // 2][:, cols],
+                rhs=codes["w", c][:].bitcast(FP8X4),
+                rhs_scale=scales["w", c][:],
+                start=True,
+                stop=True,
+            )
+
+        def drain_hidden(i, c, eng="S"):
+            g, t = divmod(i, PACK)
+            if (g, c) not in hidden_bf:
+                hidden_bf[g, c] = keep.tile([P, PACK, PASS], BF16, name="hidden%d_%d" % (g, c), align_bytes=64)
+            dst = hidden_bf[g, c][:, t, :].rearrange("p (u m e) -> p u m e", u=2, e=2)
+            src = pend["H", i, c][:].rearrange("p (m u e) -> p u m e", u=2, e=2)
+            if eng == "V":
+                nc.vector.tensor_relu(out=dst, in_=src)
+            else:
+                nc.scalar.activation(out=dst, in_=src, func=ACT.Relu)
+
+        def routed_pass(i, n, g, held=None):
+            if g == 0:
+                pend["R", i, n] = next_bank() if held is None else bank_tile(held)
+            cols = slice(P * (i % 2), P * (i % 2 + 1))
+            nc.tensor.matmul_mx(
+                out=pend["R", i, n][:],
+                lhsT=codes["t", i // 2, g][:, cols].bitcast(FP8X4),
+                lhsT_scale=scales["t", i // 2, g][:, cols],
+                rhs=raw["r", g][:, 2 * PASS * n : 2 * PASS * (n + 1)].bitcast(FP4X4),
+                rhs_scale=r_scales[:, g, PASS * n : PASS * (n + 1)],
+                start=(g == 0),
+                stop=(g == CHUNKS - 1),
+            )
+
+        def routed(i, n):
+            for g in range(CHUNKS):
+                routed_pass(i, n, g)
+
+        def drain_routed(i, n, eng="S"):
+            result[i, n] = keep.tile([P, PASS], F32, name="result%d_%d" % (i, n))
+            if eng == "V":
+                nc.vector.tensor_scalar_mul(result[i, n][:], pend["R", i, n][:], gate_f32[:, i : i + 1])
+            else:
+                nc.scalar.activation(
+                    out=result[i, n][:], in_=pend["R", i, n][:], func=ACT.Copy, scale=gate_f32[:, i : i + 1]
+                )
+
+        def shared(i, n):
+            bank = next_bank()
+            pend["S", i, n] = bank
+            for g in range(GROUPS):
+                cols = slice(P * g, P * (g + 1))
+                nc.tensor.matmul_mx(
+                    out=bank[:],
+                    lhsT=codes["m", i][:, cols].bitcast(FP8X4),
+                    lhsT_scale=scales["m", i][:, cols],
+                    rhs=codes["h", g, n][:].bitcast(FP8X4),
+                    rhs_scale=scales["h", g, n][:],
+                    start=(g == 0),
+                    stop=(g == GROUPS - 1),
+                )
+
+        def finish(i, n):
+            total = result[i, n][:].rearrange("p (m u e) -> p m u e", u=2, e=2)
+            nc.vector.tensor_tensor(
+                out=total,
+                in0=pend["S", i, n][:].rearrange("p (u m e) -> p m u e", u=2, e=2),
+                in1=total,
+                op=ALU.add,
+            )
+            nc.sync.dma_start(
+                out=out_rows[i // PACK, i % PACK, :, n * PASS : (n + 1) * PASS], in_=result[i, n][:]
+            )
+
+        load_w(0); load_x(0); load_w(1); load_w(2); load_scales(); load_r(0); load_x(1); load_r(1); load_r(2); load_gate()
+        load_x(2); load_x(3)
+        for p in (0,2,1,3): load_mix(p)
+        interleave_w(0,'V',0,320); interleave_w(0,'S',320,512)
+        turn(('x',0)); drain_turn(('x',0)); quantize(('w',0)); quantize(('x',0));
+        interleave_w(1,'V',0,320); interleave_w(1,'S',320,512)
+        hidden(0,0); hidden(1,0); drain_hidden(0,0); drain_hidden(1,0)
+        quantize(('w',1))
+        interleave_w(2)
+        turn(('t',0,0)); drain_turn(('t',0,0))
+        hidden(0,1); hidden(1,1); drain_hidden(0,1); drain_hidden(1,1)
+        quantize(('w',2)); quantize(('t',0,0))
+        turn(('t',0,1)); turn(('x',1)); drain_turn(('t',0,1),'V'); drain_turn(('x',1))
+        hidden(0,2); hidden(1,2); drain_hidden(0,2); drain_hidden(1,2)
+        for n in range(3): routed_pass(0,n,0,n)
+        quantize(('t',0,1)); quantize(('x',1))
+        turn(('t',0,2)); drain_turn(('t',0,2),'V')
+        for n in range(3): routed_pass(0,n,1)
+        hidden(2,0); hidden(3,0); drain_hidden(2,0); drain_hidden(3,0)
+        quantize(('t',0,2))
+        hidden(2,1); hidden(3,1); drain_hidden(2,1,'V'); drain_hidden(3,1,'V')
+        for n in range(3): routed_pass(0,n,2)
+        for n in range(3): drain_routed(0,n)
+        free.extend([0,1,2])
+        hidden(2,2); hidden(3,2); drain_hidden(2,2,'V'); drain_hidden(3,2,'V')
+        turn(('t',1,0)); turn(('t',1,1)); drain_turn(('t',1,0)); drain_turn(('t',1,1))
+        routed(1,0); drain_routed(1,0);
+        routed(1,1); drain_routed(1,1); quantize(('t',1,0)); quantize(('t',1,1))
+        turn(('t',1,2)); turn(('x',2)); turn(('x',3)); drain_turn(('t',1,2),'V'); drain_turn(('x',2),'V'); drain_turn(('x',3));
+        routed(1,2); drain_routed(1,2); quantize(('t',1,2)); quantize(('x',2)); quantize(('x',3))
+        steps=[(i,n) for i in (2,3) for n in range(3)]
+        for s,(i,n) in enumerate(steps):
+            c,p = s//2, 2+s%2
+            hidden(2*p,c); hidden(2*p+1,c); drain_hidden(2*p,c); drain_hidden(2*p+1,c,'S' if s%2==0 else 'V')
+            if s%2==0: interleave_h(0,c)
+            routed(i,n); drain_routed(i,n)
+            if s%2==0: quantize(('h',0,c))
+            if s in (1,3,5):
+                a=('t',2,s//2); b=('m',(0,1,4)[s//2])
+                turn(a); turn(b); drain_turn(a); drain_turn(b,'V'); quantize(a); quantize(b)
+        interleave_h(1,0)
+        seq=[(j,n) for p in (2,3) for n in range(3) for j in (2*p,2*p+1)]
+        extra={0:[('m',5)],1:[('t',3,0),('t',3,1)],3:[('t',3,2),('m',2)],5:[('m',3),('m',6)],6:[('m',7)]}
+        prev=None
+        for s,(j,n) in enumerate(seq):
+            routed(j,n); drain_routed(j,n)
+            if s==0: quantize(('h',1,0)); interleave_h(1,1)
+            if s==1: quantize(('h',1,1))
+            if s==2: interleave_h(1,2)
+            if s==3: quantize(('h',1,2))
+            for key in extra.get(s,[]): turn(key)
+            for key in extra.get(s,[]): drain_turn(key)
+            if prev:
+                shared(prev[0]-4,prev[1]); finish(prev[0]-4,prev[1])
+                shared(*prev); finish(*prev)
+            for key in extra.get(s,[]): quantize(key)
+            prev=(j,n)
+        shared(prev[0]-4,prev[1]); finish(prev[0]-4,prev[1])
+        shared(*prev); finish(*prev)

@@ -22,7 +22,6 @@ PASS = P * PACK
 GROUPS = M // PASS
 CHUNKS = F // PASS
 BANKS = 8
-HELD = 3
 
 
 def tile_mixer_expert_pair_s8_kernel(tc, x, w_in, mix, gate, routed_words, routed_scales, out):
@@ -44,16 +43,19 @@ def tile_mixer_expert_pair_s8_kernel(tc, x, w_in, mix, gate, routed_words, route
         scales = {}
         hidden_bf = {}
         result = {}
-        free = list(range(HELD, BANKS))
+        free = list(range(BANKS))
+        bank_of = {}
 
-        def bank_tile(index):
-            return psum.tile([P, PASS], F32, name="bank%d" % index, tag="bank%d" % index)
-
-        def next_bank():
+        def take_bank(key):
             index = free[0]
             free.remove(index)
-            free.append(index)
-            return bank_tile(index)
+            bank_of[key] = index
+            pend[key] = psum.tile([P, PASS], F32, name="bank%d" % index, tag="bank%d" % index)
+            return pend[key]
+
+        def release_bank(key):
+            free.append(bank_of[key])
+            return pend[key]
 
         identity = keep.tile([P, P], F32, name="identity")
         r_scales = keep.tile([P, CHUNKS, F], U8, name="r_scales", align_bytes=64)
@@ -128,16 +130,23 @@ def tile_mixer_expert_pair_s8_kernel(tc, x, w_in, mix, gate, routed_words, route
                 in_=src[:].rearrange("p c t -> p (c t)"),
             )
 
+        def order_mix(i, eng):
+            raw["ordered", i] = stage.tile([P, PASS], F32, name="ordered", tag="ordered", bufs=8)
+            row = raw["m", i // 2][:, i % 2, :].bitcast(F32)
+            copy_on(
+                eng,
+                raw["ordered", i][:].rearrange("p (a u m) -> p a u m", a=2, u=2),
+                row.rearrange("p (a m u) -> p a u m", a=2, u=2),
+            )
+
         def turn(key):
-            bank = next_bank()
-            pend[key] = bank
+            bank = take_bank(key)
             for a in range(2):
                 for u in range(2):
                     if key[0] == "x":
                         words = raw[key][:, a, :].bitcast(F32)[:, u : 2 * P : 2]
                     elif key[0] == "m":
-                        row = raw["m", key[1] // 2][:, key[1] % 2, :].bitcast(F32)
-                        words = row[:, 2 * P * a + u : 2 * P * (a + 1) : 2]
+                        words = raw["ordered", key[1]][:, (2 * a + u) * P : (2 * a + u + 1) * P]
                     else:
                         tile_index = 2 * key[1] + a
                         row = hidden_bf[tile_index // PACK, key[2]][:, tile_index % PACK, :].bitcast(F32)
@@ -146,8 +155,8 @@ def tile_mixer_expert_pair_s8_kernel(tc, x, w_in, mix, gate, routed_words, route
                     nc.tensor.transpose(bank[:, slot * P : (slot + 1) * P], words, identity[:])
 
         def drain_turn(key, eng="S"):
-            bank = pend[key]
-            pend[key] = stage.tile([P, 2 * P, PACK], BF16, name="turned", tag="turned", bufs=4, align_bytes=64)
+            bank = release_bank(key)
+            pend[key] = stage.tile([P, 2 * P, PACK], BF16, name="turned", tag="turned", bufs=8, align_bytes=64)
             dst = pend[key][:].rearrange("p c t -> p (c t)").bitcast(F32)
             copy_on(
                 eng,
@@ -156,8 +165,7 @@ def tile_mixer_expert_pair_s8_kernel(tc, x, w_in, mix, gate, routed_words, route
             )
 
         def hidden(i, c):
-            bank = next_bank()
-            pend["H", i, c] = bank
+            bank = take_bank(("H", i, c))
             cols = slice(P * (i % 2), P * (i % 2 + 1))
             nc.tensor.matmul_mx(
                 out=bank[:],
@@ -174,15 +182,15 @@ def tile_mixer_expert_pair_s8_kernel(tc, x, w_in, mix, gate, routed_words, route
             if (g, c) not in hidden_bf:
                 hidden_bf[g, c] = keep.tile([P, PACK, PASS], BF16, name="hidden%d_%d" % (g, c), align_bytes=64)
             dst = hidden_bf[g, c][:, t, :].rearrange("p (u m e) -> p u m e", u=2, e=2)
-            src = pend["H", i, c][:].rearrange("p (m u e) -> p u m e", u=2, e=2)
+            src = release_bank(("H", i, c))[:].rearrange("p (m u e) -> p u m e", u=2, e=2)
             if eng == "V":
                 nc.vector.tensor_relu(out=dst, in_=src)
             else:
                 nc.scalar.activation(out=dst, in_=src, func=ACT.Relu)
 
-        def routed_pass(i, n, g, held=None):
+        def routed_pass(i, n, g):
             if g == 0:
-                pend["R", i, n] = next_bank() if held is None else bank_tile(held)
+                take_bank(("R", i, n))
             cols = slice(P * (i % 2), P * (i % 2 + 1))
             nc.tensor.matmul_mx(
                 out=pend["R", i, n][:],
@@ -200,6 +208,7 @@ def tile_mixer_expert_pair_s8_kernel(tc, x, w_in, mix, gate, routed_words, route
 
         def drain_routed(i, n, eng="S"):
             result[i, n] = keep.tile([P, PASS], F32, name="result%d_%d" % (i, n))
+            release_bank(("R", i, n))
             if eng == "V":
                 nc.vector.tensor_scalar_mul(result[i, n][:], pend["R", i, n][:], gate_f32[:, i : i + 1])
             else:
@@ -208,8 +217,7 @@ def tile_mixer_expert_pair_s8_kernel(tc, x, w_in, mix, gate, routed_words, route
                 )
 
         def shared(i, n):
-            bank = next_bank()
-            pend["S", i, n] = bank
+            bank = take_bank(("S", i, n))
             for g in range(GROUPS):
                 cols = slice(P * g, P * (g + 1))
                 nc.tensor.matmul_mx(
@@ -226,7 +234,7 @@ def tile_mixer_expert_pair_s8_kernel(tc, x, w_in, mix, gate, routed_words, route
             total = result[i, n][:].rearrange("p (m u e) -> p m u e", u=2, e=2)
             nc.vector.tensor_tensor(
                 out=total,
-                in0=pend["S", i, n][:].rearrange("p (u m e) -> p m u e", u=2, e=2),
+                in0=release_bank(("S", i, n))[:].rearrange("p (u m e) -> p m u e", u=2, e=2),
                 in1=total,
                 op=ALU.add,
             )
@@ -234,62 +242,57 @@ def tile_mixer_expert_pair_s8_kernel(tc, x, w_in, mix, gate, routed_words, route
                 out=out_rows[i // PACK, i % PACK, :, n * PASS : (n + 1) * PASS], in_=result[i, n][:]
             )
 
-        load_w(0); load_x(0); load_w(1); load_w(2); load_scales(); load_r(0); load_x(1); load_r(1); load_r(2); load_gate()
-        load_x(2); load_x(3)
-        for p in (0,2,1,3): load_mix(p)
+        load_x(0); load_x(1); load_w(0); load_x(2); load_w(1); load_x(3); load_w(2)
+        load_gate()
+        for g in range(3): load_r(g)
+        load_scales()
+        for p in range(4): load_mix(p)
+        def H(i,c,e):
+            hidden(i,c); drain_hidden(i,c,e)
+        def run(keys, engs):
+            for key in keys: turn(key)
+            for key,e in zip(keys,engs): drain_turn(key,e)
+        turn(('x',0)); turn(('x',1)); turn(('x',2)); drain_turn(('x',0),'V')
         interleave_w(0,'V',0,320); interleave_w(0,'S',320,512)
-        turn(('x',0)); drain_turn(('x',0)); quantize(('w',0)); quantize(('x',0));
+        drain_turn(('x',1),'S')
+        quantize(('x',0)); quantize(('w',0))
         interleave_w(1,'V',0,320); interleave_w(1,'S',320,512)
-        hidden(0,0); hidden(1,0); drain_hidden(0,0); drain_hidden(1,0)
-        quantize(('w',1))
-        interleave_w(2)
-        turn(('t',0,0)); drain_turn(('t',0,0))
-        hidden(0,1); hidden(1,1); drain_hidden(0,1); drain_hidden(1,1)
-        quantize(('w',2)); quantize(('t',0,0))
-        turn(('t',0,1)); turn(('x',1)); drain_turn(('t',0,1),'V'); drain_turn(('x',1))
-        hidden(0,2); hidden(1,2); drain_hidden(0,2); drain_hidden(1,2)
-        for n in range(3): routed_pass(0,n,0,n)
-        quantize(('t',0,1)); quantize(('x',1))
-        turn(('t',0,2)); drain_turn(('t',0,2),'V')
-        for n in range(3): routed_pass(0,n,1)
-        hidden(2,0); hidden(3,0); drain_hidden(2,0); drain_hidden(3,0)
-        quantize(('t',0,2))
-        hidden(2,1); hidden(3,1); drain_hidden(2,1,'V'); drain_hidden(3,1,'V')
-        for n in range(3): routed_pass(0,n,2)
-        for n in range(3): drain_routed(0,n)
-        free.extend([0,1,2])
-        hidden(2,2); hidden(3,2); drain_hidden(2,2,'V'); drain_hidden(3,2,'V')
-        turn(('t',1,0)); turn(('t',1,1)); drain_turn(('t',1,0)); drain_turn(('t',1,1))
-        routed(1,0); drain_routed(1,0);
-        routed(1,1); drain_routed(1,1); quantize(('t',1,0)); quantize(('t',1,1))
-        turn(('t',1,2)); turn(('x',2)); turn(('x',3)); drain_turn(('t',1,2),'V'); drain_turn(('x',2),'V'); drain_turn(('x',3));
-        routed(1,2); drain_routed(1,2); quantize(('t',1,2)); quantize(('x',2)); quantize(('x',3))
-        steps=[(i,n) for i in (2,3) for n in range(3)]
+        drain_turn(('x',2),'S')
+        quantize(('x',1)); quantize(('w',1)); quantize(('x',2))
+        H(0,0,'S')
+        turn(('x',3))
+        interleave_w(2,'V',0,448); interleave_w(2,'S',448,512)
+        drain_turn(('x',3),'S')
+        quantize(('x',3)); quantize(('w',2))
+        order=[(1,0),(0,1),(1,1),(2,0),(3,0),(2,1),(3,1),(4,0),(5,0),(0,2),(1,2),(2,2),(3,2),(4,1),(5,1),(6,0),(7,0),(6,1),(7,1)]
+        for j,(i,c) in enumerate(order): H(i,c,'S' if j<2 else 'VS'[j%2])
+        first=[('t',0,0),('t',0,1),('t',0,2),('t',1,0),('t',1,1),('t',1,2)]
+        run(first[:4],'SVSV')
+        for i in range(4,8): hidden(i,2)
+        for key in first[:3]: quantize(key)
+        for i in range(4,8): drain_hidden(i,2,'S')
+        run(first[4:]+[('t',2,0),('t',2,1)],'VSVS')
+        steps=[(i,n) for i in range(6) for n in range(3)]
+        runs={3:[('t',2,2),('t',3,0),('t',3,1),('t',3,2)], 8:[('m',j) for j in range(4)], 13:[('m',j) for j in range(4,8)]}
+        wide={6:(0,0),11:(1,0),15:(0,1)}
         for s,(i,n) in enumerate(steps):
-            c,p = s//2, 2+s%2
-            hidden(2*p,c); hidden(2*p+1,c); drain_hidden(2*p,c); drain_hidden(2*p+1,c,'S' if s%2==0 else 'V')
-            if s%2==0: interleave_h(0,c)
-            routed(i,n); drain_routed(i,n)
-            if s%2==0: quantize(('h',0,c))
-            if s in (1,3,5):
-                a=('t',2,s//2); b=('m',(0,1,4)[s//2])
-                turn(a); turn(b); drain_turn(a); drain_turn(b,'V'); quantize(a); quantize(b)
-        interleave_h(1,0)
-        seq=[(j,n) for p in (2,3) for n in range(3) for j in (2*p,2*p+1)]
-        extra={0:[('m',5)],1:[('t',3,0),('t',3,1)],3:[('t',3,2),('m',2)],5:[('m',3),('m',6)],6:[('m',7)]}
-        prev=None
-        for s,(j,n) in enumerate(seq):
-            routed(j,n); drain_routed(j,n)
-            if s==0: quantize(('h',1,0)); interleave_h(1,1)
-            if s==1: quantize(('h',1,1))
-            if s==2: interleave_h(1,2)
-            if s==3: quantize(('h',1,2))
-            for key in extra.get(s,[]): turn(key)
-            for key in extra.get(s,[]): drain_turn(key)
-            if prev:
-                shared(prev[0]-4,prev[1]); finish(prev[0]-4,prev[1])
-                shared(*prev); finish(*prev)
-            for key in extra.get(s,[]): quantize(key)
-            prev=(j,n)
-        shared(prev[0]-4,prev[1]); finish(prev[0]-4,prev[1])
-        shared(*prev); finish(*prev)
+            routed(i,n)
+            if s==0:
+                for key in first[3:]+[('t',2,0),('t',2,1)]: quantize(key)
+            if s in runs: run(runs[s],'SVSV')
+            if s in wide: interleave_h(*wide[s])
+            drain_routed(i,n,'S')
+            if s==16: interleave_h(1,1,'S')
+            if s-1 in runs:
+                for key in runs[s-1]: quantize(key)
+            if s-1 in wide: quantize(('h',)+wide[s-1])
+            if 1<=s<=8: order_mix(s-1,'V')
+        for n in range(3):
+            shared(0,n); finish(0,n); shared(1,n); finish(1,n)
+            routed(6,n); drain_routed(6,n)
+            if n==0: quantize(('h',1,1)); interleave_h(0,2,'S')
+            if n==1: quantize(('h',1,2))
+            shared(2,n); finish(2,n); shared(3,n); finish(3,n); shared(4,n); finish(4,n)
+            routed(7,n); drain_routed(7,n)
+            if n==0: quantize(('h',0,2)); interleave_h(1,2,'S')
+            shared(5,n); finish(5,n); shared(6,n); finish(6,n); shared(7,n); finish(7,n)

@@ -82,6 +82,13 @@ def tile_mixer_expert_pair_s8_kernel(tc, x, w_in, mix, gate, routed_words, route
             first = 2 * (pair % 2)
             nc.sync.dma_start(out=raw["m", pair][:], in_=mix_rows[pair // 2, :, first : first + 2, :])
 
+        def load_mix_quadrants():
+            raw["mq"] = keep.tile([P, 4, 2 * PACK, P], BF16, name="mix_quadrants")
+            rows = mix[PASS:, :].rearrange("(b j t) (g q w) -> b q j (t g) w", b=4, t=PACK, g=GROUPS, q=4)
+            for b in range(4):
+                for q in (0, 2, 1, 3):
+                    nc.sync.dma_start(out=raw["mq"][32 * q : 32 * (q + 1), b, :, :], in_=rows[b, q])
+
         def load_r(g):
             raw["r", g] = keep.tile([P, 2 * F], U8, name="r_words%d" % g, align_bytes=64)
             nc.sync.dma_start(out=raw["r", g][:].bitcast(I32), in_=routed_words[g].bitcast(I32))
@@ -131,7 +138,16 @@ def tile_mixer_expert_pair_s8_kernel(tc, x, w_in, mix, gate, routed_words, route
             )
 
         def order_mix(i, eng):
-            raw["ordered", i] = stage.tile([P, PASS], F32, name="ordered", tag="ordered", bufs=8)
+            raw["ordered", i] = stage.tile([P, PASS], F32, name="ordered", tag="ordered", bufs=8, align_bytes=64)
+            if i >= PACK:
+                t = i - PACK
+                words = raw["mq"][:, :, 2 * t : 2 * t + 2, :].bitcast(F32)
+                copy_on(
+                    eng,
+                    raw["ordered", i][:].rearrange("p (g u b i) -> p g u b i", g=2, u=2, b=4),
+                    words.rearrange("p b g (i u) -> p g u b i", u=2),
+                )
+                return
             row = raw["m", i // 2][:, i % 2, :].bitcast(F32)
             copy_on(
                 eng,
@@ -140,6 +156,10 @@ def tile_mixer_expert_pair_s8_kernel(tc, x, w_in, mix, gate, routed_words, route
             )
 
         def turn(key):
+            if key[0] == "m" and key[1] >= PACK:
+                pend[key] = stage.tile([P, PASS], F32, name="blocks", tag="blocks", bufs=3, align_bytes=64)
+                nc.vector.transpose(pend[key][:], raw["ordered", key[1]][:])
+                return
             bank = take_bank(key)
             for a in range(2):
                 for u in range(2):
@@ -155,7 +175,7 @@ def tile_mixer_expert_pair_s8_kernel(tc, x, w_in, mix, gate, routed_words, route
                     nc.tensor.transpose(bank[:, slot * P : (slot + 1) * P], words, identity[:])
 
         def drain_turn(key, eng="S"):
-            bank = release_bank(key)
+            bank = release_bank(key) if key in bank_of else pend[key]
             pend[key] = stage.tile([P, 2 * P, PACK], BF16, name="turned", tag="turned", bufs=8, align_bytes=64)
             dst = pend[key][:].rearrange("p c t -> p (c t)").bitcast(F32)
             copy_on(
@@ -242,11 +262,36 @@ def tile_mixer_expert_pair_s8_kernel(tc, x, w_in, mix, gate, routed_words, route
                 out=out_rows[i // PACK, i % PACK, :, n * PASS : (n + 1) * PASS], in_=result[i, n][:]
             )
 
+        def drain_shared(i, n):
+            result[i, n] = keep.tile([P, PASS], F32, name="result%d_%d" % (i, n))
+            nc.scalar.copy(
+                out=result[i, n][:].rearrange("p (m u e) -> p m u e", u=2, e=2),
+                in_=release_bank(("S", i, n))[:].rearrange("p (u m e) -> p m u e", u=2, e=2),
+            )
+
+        def finish_routed(i, n):
+            bank = release_bank(("R", i, n))
+            for lo in (0, PASS // 2):
+                cols = slice(lo, lo + PASS // 2)
+                nc.vector.scalar_tensor_tensor(
+                    out=result[i, n][:, cols],
+                    in0=bank[:, cols],
+                    scalar=gate_f32[:, i : i + 1],
+                    in1=result[i, n][:, cols],
+                    op0=ALU.mult,
+                    op1=ALU.add,
+                )
+                nc.sync.dma_start(
+                    out=out_rows[i // PACK, i % PACK, :, n * PASS + lo : n * PASS + lo + PASS // 2],
+                    in_=result[i, n][:, cols],
+                )
+
         load_x(0); load_x(1); load_w(0); load_x(2); load_w(1); load_x(3); load_w(2)
         load_gate()
         for g in range(3): load_r(g)
         load_scales()
-        for p in range(4): load_mix(p)
+        for p in range(2): load_mix(p)
+        load_mix_quadrants()
         def H(i,c,e):
             hidden(i,c); drain_hidden(i,c,e)
         def run(keys, engs):
@@ -272,27 +317,37 @@ def tile_mixer_expert_pair_s8_kernel(tc, x, w_in, mix, gate, routed_words, route
         for key in first[:3]: quantize(key)
         for i in range(4,8): drain_hidden(i,2,'S')
         run(first[4:]+[('t',2,0),('t',2,1)],'VSVS')
-        steps=[(i,n) for i in range(6) for n in range(3)]
-        runs={3:[('t',2,2),('t',3,0),('t',3,1),('t',3,2)], 8:[('m',j) for j in range(4)], 13:[('m',j) for j in range(4,8)]}
-        wide={6:(0,0),11:(1,0),15:(0,1)}
+
+        steps=[(i,n) for i in range(4) for n in range(3)]+[(4,0),(5,0)]
+        runs={3:[('t',2,2),('t',3,0),('t',3,1),('t',3,2)], 8:[('m',j) for j in range(4)]}
+        wide={2:(0,0),5:(1,0),7:(0,1),11:(1,1)}
         for s,(i,n) in enumerate(steps):
             routed(i,n)
             if s==0:
                 for key in first[3:]+[('t',2,0),('t',2,1)]: quantize(key)
-            if s in runs: run(runs[s],'SVSV')
+            if s in runs: run(runs[s],'SVSS')
             if s in wide: interleave_h(*wide[s])
             drain_routed(i,n,'S')
-            if s==16: interleave_h(1,1,'S')
             if s-1 in runs:
                 for key in runs[s-1]: quantize(key)
             if s-1 in wide: quantize(('h',)+wide[s-1])
-            if 1<=s<=8: order_mix(s-1,'V')
-        for n in range(3):
-            shared(0,n); finish(0,n); shared(1,n); finish(1,n)
-            routed(6,n); drain_routed(6,n)
-            if n==0: quantize(('h',1,1)); interleave_h(0,2,'S')
-            if n==1: quantize(('h',1,2))
-            shared(2,n); finish(2,n); shared(3,n); finish(3,n); shared(4,n); finish(4,n)
-            routed(7,n); drain_routed(7,n)
-            if n==0: quantize(('h',0,2)); interleave_h(1,2,'S')
-            shared(5,n); finish(5,n); shared(6,n); finish(6,n); shared(7,n); finish(7,n)
+            if 1<=s<=4: order_mix(s-1,'V')
+            if s in (6,7,12,13): order_mix((6,7,12,13).index(s)+4,'S')
+            if s in (10,13): turn(('m',4+s//13))
+        def both(i,n):
+            shared(i,n); finish(i,n)
+        def gated(i,n):
+            routed(i,n); drain_routed(i,n)
+        pairs=[(0,0),(2,0),(0,1),(2,1),(4,0),(6,0),(4,1),(6,1),(0,2),(2,2)]
+        late=[(6,0),(7,0),(4,1),(5,1),(6,1),(7,1),(4,2),(5,2),(6,2)]
+        for s,(i,n) in enumerate(pairs):
+            if s<4: drain_turn(('m',4+s),'S')
+            if s in (3,5): interleave_h(s//4,2,'S')
+            both(i,n)
+            if s<2: turn(('m',6+s))
+            both(i+1,n)
+            if s<4: quantize(('m',4+s))
+            if s<9: gated(*late[s])
+            if s in (4,6): quantize(('h',s//6,2))
+        both(4,2); shared(7,2); drain_shared(7,2)
+        both(5,2); both(6,2); routed(7,2); finish_routed(7,2)

@@ -19,9 +19,23 @@ ALU = mybir.AluOpType
 P = 128
 PACK = 4
 PASS = P * PACK
+QUADRANT = 32
 GROUPS = M // PASS
+TILES = M // P
 CHUNKS = F // PASS
 BANKS = 8
+
+VECTOR, SCALAR = "vector", "scalar"
+W_COLUMNS_ON_VECTOR = (320, 320, 448)
+
+ROUTED_ONLY_STEPS = 16
+FIRST_MIXED_STEP = 18
+LAST_TURN_STEP = 5
+MIX_START = 4
+MIX_TRANSPOSE_LAG, MIX_PAIR_LAG, MIX_QUANTIZE_LAG = 1, 3, 5
+INTERLEAVE_ON_VECTOR = {2: (1, 0), 7: (1, 1)}
+INTERLEAVE_ON_SCALAR = {18: (0, 2), 19: (1, 2)}
+QUANTIZE_H = {1: (0, 0), 2: (0, 1), 3: (1, 0), 8: (1, 1), 20: (0, 2), 21: (1, 2)}
 
 
 def tile_mixer_expert_pair_s8_kernel(tc, x, w_in, mix, gate, routed_words, routed_scales, out):
@@ -33,321 +47,365 @@ def tile_mixer_expert_pair_s8_kernel(tc, x, w_in, mix, gate, routed_words, route
         ctx.enter_context(tc.manual_schedule())
 
         x_rows = x.rearrange("(g p t) k -> g p t k", g=GROUPS, t=PACK)
-        mix_rows = mix.rearrange("(g p t) k -> g p t k", g=GROUPS, t=PACK)
         out_rows = out.rearrange("(g p t) f -> g t p f", g=GROUPS, t=PACK)
         w_rows = w_in.rearrange("(p j) f -> p j f", j=PACK)
 
-        raw = {}
-        pend = {}
+        loaded = {}
+        turned = {}
+        grouped = {}
         codes = {}
         scales = {}
-        hidden_bf = {}
+        hidden = {}
+        ordered = {}
         result = {}
-        free = list(range(BANKS))
-        bank_of = {}
+
+        free_banks = list(range(BANKS))
+        held = {}
 
         def take_bank(key):
-            index = free[0]
-            free.remove(index)
-            bank_of[key] = index
-            pend[key] = psum.tile([P, PASS], F32, name="bank%d" % index, tag="bank%d" % index)
-            return pend[key]
+            index = free_banks[0]
+            free_banks.remove(index)
+            bank = psum.tile([P, PASS], F32, name="bank%d" % index, tag="bank%d" % index)
+            held[key] = (index, bank)
+            return bank
 
         def release_bank(key):
-            free.append(bank_of[key])
-            return pend[key]
+            index, bank = held[key]
+            free_banks.append(index)
+            return bank
 
         identity = keep.tile([P, P], F32, name="identity")
         r_scales = keep.tile([P, CHUNKS, F], U8, name="r_scales", align_bytes=64)
-        gate_bf = keep.tile([P, GROUPS, PACK], BF16, name="gate_bf")
-        gate_f32 = keep.tile([P, GROUPS * PACK], F32, name="gate_f32")
-        warm_in = keep.tile([P, 1], F32, name="warm_in")
-        warm_out = keep.tile([P, 1], F32, name="warm_out")
-        nc.vector.memset(warm_in[:], 0.0)
-        nc.scalar.activation(out=warm_out[:], in_=warm_in[:], func=ACT.Relu)
+        gate_bf16 = keep.tile([P, GROUPS, PACK], BF16, name="gate_bf16")
+        gate_f32 = keep.tile([P, TILES], F32, name="gate_f32")
+        first_in = keep.tile([P, 1], F32, name="first_in")
+        first_out = keep.tile([P, 1], F32, name="first_out")
+
+        nc.vector.memset(first_in[:], 0.0)
+        nc.scalar.activation(out=first_out[:], in_=first_in[:], func=ACT.Relu)
         make_identity(nc, identity[:])
         nc.gpsimd.memset(r_scales[:].rearrange("p g n -> p (g n)").bitcast(I32), 0)
 
-        def load_w(c):
-            raw["w", c] = keep.tile([P, PACK, PASS], BF16, name="w_raw%d" % c)
-            nc.sync.dma_start(out=raw["w", c][:], in_=w_rows[:, :, c * PASS : (c + 1) * PASS])
-
         def load_x(pair):
-            raw["x", pair] = keep.tile([P, 2, K], BF16, name="x_raw%d" % pair)
-            first = 2 * (pair % 2)
-            nc.sync.dma_start(out=raw["x", pair][:], in_=x_rows[pair // 2, :, first : first + 2, :])
+            loaded["x", pair] = keep.tile([P, 2, K], BF16, name="x_rows%d" % pair)
+            t = 2 * (pair % 2)
+            nc.sync.dma_start(out=loaded["x", pair][:], in_=x_rows[pair // 2, :, t : t + 2, :])
 
-        def load_mix(pair):
-            raw["m", pair] = keep.tile([P, 2, M], BF16, name="mix_raw%d" % pair)
-            first = 2 * (pair % 2)
-            nc.sync.dma_start(out=raw["m", pair][:], in_=mix_rows[pair // 2, :, first : first + 2, :])
+        def load_w(c):
+            loaded["w", c] = keep.tile([P, PACK, PASS], BF16, name="w_rows%d" % c)
+            nc.sync.dma_start(out=loaded["w", c][:], in_=w_rows[:, :, c * PASS : (c + 1) * PASS])
 
-        def load_mix_quadrants():
-            raw["mq"] = keep.tile([P, 4, 2 * PACK, P], BF16, name="mix_quadrants")
-            rows = mix[PASS:, :].rearrange("(b j t) (g q w) -> b q j (t g) w", b=4, t=PACK, g=GROUPS, q=4)
-            for b in range(4):
-                for q in (0, 2, 1, 3):
-                    nc.sync.dma_start(out=raw["mq"][32 * q : 32 * (q + 1), b, :, :], in_=rows[b, q])
+        def load_gate():
+            nc.sync.dma_start(out=gate_bf16[:], in_=gate.rearrange("(g p t) -> p g t", g=GROUPS, t=PACK))
+            nc.gpsimd.tensor_copy(out=gate_f32[:], in_=gate_bf16[:].rearrange("p g t -> p (g t)"))
 
-        def load_r(g):
-            raw["r", g] = keep.tile([P, 2 * F], U8, name="r_words%d" % g, align_bytes=64)
-            nc.sync.dma_start(out=raw["r", g][:].bitcast(I32), in_=routed_words[g].bitcast(I32))
-
-        def load_scales():
+        def load_routed_weight():
+            for g in range(CHUNKS):
+                loaded["r", g] = keep.tile([P, 2 * F], U8, name="r_words%d" % g, align_bytes=64)
+                nc.sync.dma_start(out=loaded["r", g][:].bitcast(I32), in_=routed_words[g].bitcast(I32))
             for q in range(4):
                 nc.sync.dma_start(
-                    out=r_scales[32 * q : 32 * q + 4, :, :].bitcast(I32),
+                    out=r_scales[QUADRANT * q : QUADRANT * q + 4, :, :].bitcast(I32),
                     in_=routed_scales[:, 4 * q : 4 * q + 4, :].rearrange("g r n -> r g n").bitcast(I32),
                 )
 
-        def load_gate():
-            nc.sync.dma_start(out=gate_bf[:], in_=gate.rearrange("(g p t) -> p g t", g=GROUPS, t=PACK))
-            nc.gpsimd.tensor_copy(out=gate_f32[:], in_=gate_bf[:].rearrange("p g t -> p (g t)"))
+        def load_mix(group):
+            loaded["mix", group] = keep.tile([P, 4, PACK * GROUPS, P], BF16, name="mix_rows%d" % group)
+            rows = mix[group * PASS : (group + 1) * PASS, :].rearrange(
+                "(b j t) (g q w) -> b q j (t g) w", b=4, t=PACK, g=GROUPS, q=4
+            )
+            for b in range(4):
+                for q in (0, 2, 1, 3):
+                    nc.sync.dma_start(
+                        out=loaded["mix", group][QUADRANT * q : QUADRANT * (q + 1), b, :, :], in_=rows[b, q]
+                    )
 
-        def copy_on(eng, dst, src):
-            if eng == "V":
+        def copy_on(engine, dst, src):
+            if engine == VECTOR:
                 nc.vector.tensor_copy(out=dst, in_=src)
             else:
                 nc.scalar.copy(out=dst, in_=src)
 
-        def interleave(key, src, eng, lo, hi):
-            if lo == 0:
-                pend[key] = stage.tile([P, PASS, PACK], BF16, name="wide", tag="wide", bufs=3, align_bytes=64)
+        def new_wide_group(key):
+            grouped[key] = stage.tile([P, PASS, PACK], BF16, name="wide", tag="wide", bufs=3, align_bytes=64)
+
+        def interleave(key, src, engine, lo, hi):
             copy_on(
-                eng,
-                pend[key][:, lo:hi, :].rearrange("p (c i) t -> p c t i", i=4),
+                engine,
+                grouped[key][:, lo:hi, :].rearrange("p (c i) t -> p c t i", i=4),
                 src[:, :, lo:hi].rearrange("p t (c i) -> p c t i", i=4),
             )
 
-        def interleave_w(c, eng="V", lo=0, hi=PASS):
-            interleave(("w", c), raw["w", c], eng, lo, hi)
+        def interleave_w(c):
+            new_wide_group(("w", c))
+            interleave(("w", c), loaded["w", c], VECTOR, 0, W_COLUMNS_ON_VECTOR[c])
+            interleave(("w", c), loaded["w", c], SCALAR, W_COLUMNS_ON_VECTOR[c], PASS)
 
-        def interleave_h(g, c, eng="V"):
-            interleave(("h", g, c), hidden_bf[g, c], eng, 0, PASS)
+        def interleave_h(g, c, engine):
+            new_wide_group(("h", g, c))
+            interleave(("h", g, c), hidden[g, c], engine, 0, PASS)
+
+        def interleave_h_on_gpsimd(g, c):
+            new_wide_group(("h", g, c))
+            for lo in range(0, PASS, P):
+                nc.gpsimd.tensor_scalar(
+                    out=grouped["h", g, c][:, lo : lo + P, :],
+                    in0=hidden[g, c][:, :, lo : lo + P].rearrange("p t c -> p c t"),
+                    scalar1=1.0,
+                    scalar2=0.0,
+                    op0=ALU.mult,
+                    op1=ALU.add,
+                )
 
         def quantize(key):
-            src = pend[key]
-            width = src.shape[1]
+            columns = grouped[key].shape[1]
             label = "_".join(str(part) for part in key)
-            codes[key] = keep.tile([P, width], U32, name="codes_" + label, align_bytes=64)
-            scales[key] = keep.tile([P, width], U8, name="scales_" + label, align_bytes=64)
+            codes[key] = keep.tile([P, columns], U32, name="codes_" + label, align_bytes=64)
+            scales[key] = keep.tile([P, columns], U8, name="scales_" + label, align_bytes=64)
             nc.vector.quantize_mx(
                 out=codes[key][:].bitcast(FP8X4),
                 scales=scales[key][:],
-                in_=src[:].rearrange("p c t -> p (c t)"),
+                in_=grouped[key][:].rearrange("p c t -> p (c t)"),
             )
 
-        def order_mix(i, eng):
-            raw["ordered", i] = stage.tile([P, PASS], F32, name="ordered", tag="ordered", bufs=8, align_bytes=64)
-            if i >= PACK:
-                t = i - PACK
-                words = raw["mq"][:, :, 2 * t : 2 * t + 2, :].bitcast(F32)
-                copy_on(
-                    eng,
-                    raw["ordered", i][:].rearrange("p (g u b i) -> p g u b i", g=2, u=2, b=4),
-                    words.rearrange("p b g (i u) -> p g u b i", u=2),
-                )
-                return
-            row = raw["m", i // 2][:, i % 2, :].bitcast(F32)
-            copy_on(
-                eng,
-                raw["ordered", i][:].rearrange("p (a u m) -> p a u m", a=2, u=2),
-                row.rearrange("p (a m u) -> p a u m", a=2, u=2),
-            )
-
-        def turn(key):
-            if key[0] == "m" and key[1] >= PACK:
-                pend[key] = stage.tile([P, PASS], F32, name="blocks", tag="blocks", bufs=3, align_bytes=64)
-                nc.vector.transpose(pend[key][:], raw["ordered", key[1]][:])
-                return
-            bank = take_bank(key)
-            for a in range(2):
+        def transpose_x(pair):
+            bank = take_bank(("x", pair))
+            for half in range(2):
+                words = loaded["x", pair][:, half, :].bitcast(F32)
                 for u in range(2):
-                    if key[0] == "x":
-                        words = raw[key][:, a, :].bitcast(F32)[:, u : 2 * P : 2]
-                    elif key[0] == "m":
-                        words = raw["ordered", key[1]][:, (2 * a + u) * P : (2 * a + u + 1) * P]
-                    else:
-                        tile_index = 2 * key[1] + a
-                        row = hidden_bf[tile_index // PACK, key[2]][:, tile_index % PACK, :].bitcast(F32)
-                        words = row[:, P * u : P * (u + 1)]
-                    slot = 2 * a + u
-                    nc.tensor.transpose(bank[:, slot * P : (slot + 1) * P], words, identity[:])
+                    slot = 2 * half + u
+                    nc.tensor.transpose(bank[:, slot * P : (slot + 1) * P], words[:, u : 2 * P : 2], identity[:])
 
-        def drain_turn(key, eng="S"):
-            bank = release_bank(key) if key in bank_of else pend[key]
-            pend[key] = stage.tile([P, 2 * P, PACK], BF16, name="turned", tag="turned", bufs=8, align_bytes=64)
-            dst = pend[key][:].rearrange("p c t -> p (c t)").bitcast(F32)
-            copy_on(
-                eng,
-                dst.rearrange("p (a r u) -> p a r u", a=2, u=2),
-                bank[:].rearrange("p (a u r) -> p a r u", a=2, u=2),
+        def transpose_h(pair, c):
+            bank = take_bank(("ht", pair, c))
+            for half in range(2):
+                g, t = divmod(2 * pair + half, PACK)
+                words = hidden[g, c][:, t, :].bitcast(F32)
+                for u in range(2):
+                    slot = 2 * half + u
+                    nc.tensor.transpose(bank[:, slot * P : (slot + 1) * P], words[:, u * P : (u + 1) * P], identity[:])
+
+        def order_mix(i):
+            group, t = divmod(i, PACK)
+            ordered[i] = stage.tile([P, PASS], F32, name="ordered", tag="ordered", bufs=3, align_bytes=64)
+            words = loaded["mix", group][:, :, GROUPS * t : GROUPS * (t + 1), :].bitcast(F32)
+            nc.vector.tensor_copy(
+                out=ordered[i][:].rearrange("p (g u b w) -> p g u b w", g=GROUPS, u=2, b=4),
+                in_=words.rearrange("p b g (w u) -> p g u b w", u=2),
             )
 
-        def hidden(i, c):
-            bank = take_bank(("H", i, c))
-            cols = slice(P * (i % 2), P * (i % 2 + 1))
+        def transpose_mix(i):
+            turned["mix", i] = stage.tile([P, PASS], F32, name="blocks", tag="blocks", bufs=4, align_bytes=64)
+            nc.vector.transpose(turned["mix", i][:], ordered[i][:])
+
+        def pair_words(key, engine):
+            src = turned[key] if key in turned else release_bank(key)
+            grouped[key] = stage.tile([P, 2 * P, PACK], BF16, name="paired", tag="paired", bufs=8, align_bytes=64)
+            dst = grouped[key][:].rearrange("p c t -> p (c t)").bitcast(F32)
+            copy_on(
+                engine,
+                dst.rearrange("p (half c u) -> p half c u", half=2, u=2),
+                src[:].rearrange("p (half u c) -> p half c u", half=2, u=2),
+            )
+
+        def hidden_product(i, c):
+            tokens = slice(P * (i % 2), P * (i % 2 + 1))
             nc.tensor.matmul_mx(
-                out=bank[:],
-                lhsT=codes["x", i // 2][:, cols].bitcast(FP8X4),
-                lhsT_scale=scales["x", i // 2][:, cols],
+                out=take_bank(("hidden", i, c))[:],
+                lhsT=codes["x", i // 2][:, tokens].bitcast(FP8X4),
+                lhsT_scale=scales["x", i // 2][:, tokens],
                 rhs=codes["w", c][:].bitcast(FP8X4),
                 rhs_scale=scales["w", c][:],
                 start=True,
                 stop=True,
             )
 
-        def drain_hidden(i, c, eng="S"):
+        def relu_out(i, c, engine):
             g, t = divmod(i, PACK)
-            if (g, c) not in hidden_bf:
-                hidden_bf[g, c] = keep.tile([P, PACK, PASS], BF16, name="hidden%d_%d" % (g, c), align_bytes=64)
-            dst = hidden_bf[g, c][:, t, :].rearrange("p (u m e) -> p u m e", u=2, e=2)
-            src = release_bank(("H", i, c))[:].rearrange("p (m u e) -> p u m e", u=2, e=2)
-            if eng == "V":
+            if (g, c) not in hidden:
+                hidden[g, c] = keep.tile([P, PACK, PASS], BF16, name="hidden%d_%d" % (g, c), align_bytes=64)
+            dst = hidden[g, c][:, t, :].rearrange("p (u m e) -> p u m e", u=2, e=2)
+            src = release_bank(("hidden", i, c))[:].rearrange("p (m u e) -> p u m e", u=2, e=2)
+            if engine == VECTOR:
                 nc.vector.tensor_relu(out=dst, in_=src)
             else:
                 nc.scalar.activation(out=dst, in_=src, func=ACT.Relu)
 
-        def routed_pass(i, n, g):
-            if g == 0:
-                take_bank(("R", i, n))
-            cols = slice(P * (i % 2), P * (i % 2 + 1))
-            nc.tensor.matmul_mx(
-                out=pend["R", i, n][:],
-                lhsT=codes["t", i // 2, g][:, cols].bitcast(FP8X4),
-                lhsT_scale=scales["t", i // 2, g][:, cols],
-                rhs=raw["r", g][:, 2 * PASS * n : 2 * PASS * (n + 1)].bitcast(FP4X4),
-                rhs_scale=r_scales[:, g, PASS * n : PASS * (n + 1)],
-                start=(g == 0),
-                stop=(g == CHUNKS - 1),
-            )
-
-        def routed(i, n):
+        def routed_product(i, n):
+            bank = take_bank(("routed", i, n))
+            tokens = slice(P * (i % 2), P * (i % 2 + 1))
             for g in range(CHUNKS):
-                routed_pass(i, n, g)
-
-        def drain_routed(i, n, eng="S"):
-            result[i, n] = keep.tile([P, PASS], F32, name="result%d_%d" % (i, n))
-            release_bank(("R", i, n))
-            if eng == "V":
-                nc.vector.tensor_scalar_mul(result[i, n][:], pend["R", i, n][:], gate_f32[:, i : i + 1])
-            else:
-                nc.scalar.activation(
-                    out=result[i, n][:], in_=pend["R", i, n][:], func=ACT.Copy, scale=gate_f32[:, i : i + 1]
-                )
-
-        def shared(i, n):
-            bank = take_bank(("S", i, n))
-            for g in range(GROUPS):
-                cols = slice(P * g, P * (g + 1))
                 nc.tensor.matmul_mx(
                     out=bank[:],
-                    lhsT=codes["m", i][:, cols].bitcast(FP8X4),
-                    lhsT_scale=scales["m", i][:, cols],
+                    lhsT=codes["ht", i // 2, g][:, tokens].bitcast(FP8X4),
+                    lhsT_scale=scales["ht", i // 2, g][:, tokens],
+                    rhs=loaded["r", g][:, 2 * PASS * n : 2 * PASS * (n + 1)].bitcast(FP4X4),
+                    rhs_scale=r_scales[:, g, PASS * n : PASS * (n + 1)],
+                    start=(g == 0),
+                    stop=(g == CHUNKS - 1),
+                )
+
+        def shared_product(i, n):
+            bank = take_bank(("shared", i, n))
+            for g in range(GROUPS):
+                tokens = slice(P * g, P * (g + 1))
+                nc.tensor.matmul_mx(
+                    out=bank[:],
+                    lhsT=codes["mix", i][:, tokens].bitcast(FP8X4),
+                    lhsT_scale=scales["mix", i][:, tokens],
                     rhs=codes["h", g, n][:].bitcast(FP8X4),
                     rhs_scale=scales["h", g, n][:],
                     start=(g == 0),
                     stop=(g == GROUPS - 1),
                 )
 
-        def finish(i, n):
+        def gate_routed(i, n):
+            result[i, n] = keep.tile([P, PASS], F32, name="result%d_%d" % (i, n))
+            nc.scalar.activation(
+                out=result[i, n][:],
+                in_=release_bank(("routed", i, n))[:],
+                func=ACT.Copy,
+                scale=gate_f32[:, i : i + 1],
+            )
+
+        def store(i, n, lo, hi):
+            nc.sync.dma_start(
+                out=out_rows[i // PACK, i % PACK, :, n * PASS + lo : n * PASS + hi], in_=result[i, n][:, lo:hi]
+            )
+
+        def add_shared_and_store(i, n):
+            shared_product(i, n)
             total = result[i, n][:].rearrange("p (m u e) -> p m u e", u=2, e=2)
             nc.vector.tensor_tensor(
                 out=total,
-                in0=release_bank(("S", i, n))[:].rearrange("p (u m e) -> p m u e", u=2, e=2),
+                in0=release_bank(("shared", i, n))[:].rearrange("p (u m e) -> p m u e", u=2, e=2),
                 in1=total,
                 op=ALU.add,
             )
-            nc.sync.dma_start(
-                out=out_rows[i // PACK, i % PACK, :, n * PASS : (n + 1) * PASS], in_=result[i, n][:]
-            )
+            store(i, n, 0, PASS)
 
-        def drain_shared(i, n):
+        def copy_shared(i, n):
+            shared_product(i, n)
             result[i, n] = keep.tile([P, PASS], F32, name="result%d_%d" % (i, n))
             nc.scalar.copy(
                 out=result[i, n][:].rearrange("p (m u e) -> p m u e", u=2, e=2),
-                in_=release_bank(("S", i, n))[:].rearrange("p (u m e) -> p m u e", u=2, e=2),
+                in_=release_bank(("shared", i, n))[:].rearrange("p (u m e) -> p m u e", u=2, e=2),
             )
 
-        def finish_routed(i, n):
-            bank = release_bank(("R", i, n))
+        def add_routed_and_store(i, n):
+            routed_product(i, n)
+            bank = release_bank(("routed", i, n))
             for lo in (0, PASS // 2):
-                cols = slice(lo, lo + PASS // 2)
+                hi = lo + PASS // 2
                 nc.vector.scalar_tensor_tensor(
-                    out=result[i, n][:, cols],
-                    in0=bank[:, cols],
+                    out=result[i, n][:, lo:hi],
+                    in0=bank[:, lo:hi],
                     scalar=gate_f32[:, i : i + 1],
-                    in1=result[i, n][:, cols],
+                    in1=result[i, n][:, lo:hi],
                     op0=ALU.mult,
                     op1=ALU.add,
                 )
-                nc.sync.dma_start(
-                    out=out_rows[i // PACK, i % PACK, :, n * PASS + lo : n * PASS + lo + PASS // 2],
-                    in_=result[i, n][:, cols],
-                )
+                store(i, n, lo, hi)
 
-        load_x(0); load_x(1); load_w(0); load_x(2); load_w(1); load_x(3); load_w(2)
+        def turn_h(pieces, engines):
+            for pair, c in pieces:
+                transpose_h(pair, c)
+            for (pair, c), engine in zip(pieces, engines):
+                pair_words(("ht", pair, c), engine)
+
+        load_x(0)
+        for c in range(CHUNKS):
+            load_x(c + 1)
+            load_w(c)
         load_gate()
-        for g in range(3): load_r(g)
-        load_scales()
-        for p in range(2): load_mix(p)
-        load_mix_quadrants()
-        def H(i,c,e):
-            hidden(i,c); drain_hidden(i,c,e)
-        def run(keys, engs):
-            for key in keys: turn(key)
-            for key,e in zip(keys,engs): drain_turn(key,e)
-        turn(('x',0)); turn(('x',1)); turn(('x',2)); drain_turn(('x',0),'V')
-        interleave_w(0,'V',0,320); interleave_w(0,'S',320,512)
-        drain_turn(('x',1),'S')
-        quantize(('x',0)); quantize(('w',0))
-        interleave_w(1,'V',0,320); interleave_w(1,'S',320,512)
-        drain_turn(('x',2),'S')
-        quantize(('x',1)); quantize(('w',1)); quantize(('x',2))
-        H(0,0,'S')
-        turn(('x',3))
-        interleave_w(2,'V',0,448); interleave_w(2,'S',448,512)
-        drain_turn(('x',3),'S')
-        quantize(('x',3)); quantize(('w',2))
-        order=[(1,0),(0,1),(1,1),(2,0),(3,0),(2,1),(3,1),(4,0),(5,0),(0,2),(1,2),(2,2),(3,2),(4,1),(5,1),(6,0),(7,0),(6,1),(7,1)]
-        for j,(i,c) in enumerate(order): H(i,c,'S' if j<2 else 'VS'[j%2])
-        first=[('t',0,0),('t',0,1),('t',0,2),('t',1,0),('t',1,1),('t',1,2)]
-        run(first[:4],'SVSV')
-        for i in range(4,8): hidden(i,2)
-        for key in first[:3]: quantize(key)
-        for i in range(4,8): drain_hidden(i,2,'S')
-        run(first[4:]+[('t',2,0),('t',2,1)],'VSVS')
+        load_routed_weight()
+        for group in range(GROUPS):
+            load_mix(group)
 
-        steps=[(i,n) for i in range(4) for n in range(3)]+[(4,0),(5,0)]
-        runs={3:[('t',2,2),('t',3,0),('t',3,1),('t',3,2)], 8:[('m',j) for j in range(4)]}
-        wide={2:(0,0),5:(1,0),7:(0,1),11:(1,1)}
-        for s,(i,n) in enumerate(steps):
-            routed(i,n)
-            if s==0:
-                for key in first[3:]+[('t',2,0),('t',2,1)]: quantize(key)
-            if s in runs: run(runs[s],'SVSS')
-            if s in wide: interleave_h(*wide[s])
-            drain_routed(i,n,'S')
-            if s-1 in runs:
-                for key in runs[s-1]: quantize(key)
-            if s-1 in wide: quantize(('h',)+wide[s-1])
-            if 1<=s<=4: order_mix(s-1,'V')
-            if s in (6,7,12,13): order_mix((6,7,12,13).index(s)+4,'S')
-            if s in (10,13): turn(('m',4+s//13))
-        def both(i,n):
-            shared(i,n); finish(i,n)
-        def gated(i,n):
-            routed(i,n); drain_routed(i,n)
-        pairs=[(0,0),(2,0),(0,1),(2,1),(4,0),(6,0),(4,1),(6,1),(0,2),(2,2)]
-        late=[(6,0),(7,0),(4,1),(5,1),(6,1),(7,1),(4,2),(5,2),(6,2)]
-        for s,(i,n) in enumerate(pairs):
-            if s<4: drain_turn(('m',4+s),'S')
-            if s in (3,5): interleave_h(s//4,2,'S')
-            both(i,n)
-            if s<2: turn(('m',6+s))
-            both(i+1,n)
-            if s<4: quantize(('m',4+s))
-            if s<9: gated(*late[s])
-            if s in (4,6): quantize(('h',s//6,2))
-        both(4,2); shared(7,2); drain_shared(7,2)
-        both(5,2); both(6,2); routed(7,2); finish_routed(7,2)
+        for pair in range(3):
+            transpose_x(pair)
+        pair_words(("x", 0), VECTOR)
+        interleave_w(0)
+        pair_words(("x", 1), SCALAR)
+        quantize(("x", 0))
+        quantize(("w", 0))
+        interleave_w(1)
+        pair_words(("x", 2), SCALAR)
+        quantize(("x", 1))
+        quantize(("w", 1))
+        quantize(("x", 2))
+        hidden_product(0, 0)
+        relu_out(0, 0, SCALAR)
+        transpose_x(3)
+        interleave_w(2)
+        pair_words(("x", 3), SCALAR)
+        quantize(("x", 3))
+        quantize(("w", 2))
+
+        hidden_order = [(1, 0), (0, 1), (1, 1), (2, 0), (3, 0), (2, 1), (3, 1), (4, 0), (5, 0)]
+        hidden_order += [(i, 2) for i in range(PACK)]
+        hidden_order += [(4, 1), (5, 1), (6, 0), (7, 0), (6, 1), (7, 1)]
+        for count, (i, c) in enumerate(hidden_order):
+            hidden_product(i, c)
+            relu_out(i, c, VECTOR if count >= 2 and count % 2 == 0 else SCALAR)
+        interleave_h_on_gpsimd(0, 0)
+        interleave_h_on_gpsimd(0, 1)
+
+        pieces = [(pair, c) for pair in range(TILES // 2) for c in range(CHUNKS)]
+        turn_h(pieces[:4], (SCALAR, VECTOR, SCALAR, VECTOR))
+        for i in range(PACK, TILES):
+            hidden_product(i, 2)
+        for pair, c in pieces[:CHUNKS]:
+            quantize(("ht", pair, c))
+        for i in range(PACK, TILES):
+            relu_out(i, 2, SCALAR)
+        turn_h(pieces[4:8], (VECTOR, SCALAR, VECTOR, SCALAR))
+
+        def side_work(step):
+            entry = [MIX_START + 3 * i // 2 for i in range(TILES)]
+            if step - MIX_PAIR_LAG in entry:
+                pair_words(("mix", entry.index(step - MIX_PAIR_LAG)), SCALAR)
+            if step in entry:
+                order_mix(entry.index(step))
+            if step in INTERLEAVE_ON_SCALAR:
+                interleave_h(*INTERLEAVE_ON_SCALAR[step], SCALAR)
+            if step - MIX_TRANSPOSE_LAG in entry:
+                transpose_mix(entry.index(step - MIX_TRANSPOSE_LAG))
+            if step in QUANTIZE_H:
+                quantize(("h",) + QUANTIZE_H[step])
+            if step - MIX_QUANTIZE_LAG in entry:
+                quantize(("mix", entry.index(step - MIX_QUANTIZE_LAG)))
+
+        routed_order = [(i, n) for i in range(PACK) for n in range(CHUNKS)]
+        routed_order += [(i, n) for n in range(CHUNKS) for i in range(PACK, TILES)][:-1]
+        for step, (i, n) in enumerate(routed_order[:ROUTED_ONLY_STEPS]):
+            routed_product(i, n)
+            if step == 0:
+                for pair, c in pieces[CHUNKS:8]:
+                    quantize(("ht", pair, c))
+            if step == LAST_TURN_STEP:
+                turn_h(pieces[8:], (SCALAR,) * 4)
+            if step in INTERLEAVE_ON_VECTOR:
+                interleave_h(*INTERLEAVE_ON_VECTOR[step], VECTOR)
+            gate_routed(i, n)
+            if step == LAST_TURN_STEP + 1:
+                for pair, c in pieces[8:]:
+                    quantize(("ht", pair, c))
+            side_work(step)
+
+        last = CHUNKS - 1
+        shared_order = [(pair, n) for pair in range(TILES // 2) for n in range(last)] + [(0, last), (1, last)]
+        routed_left = routed_order[ROUTED_ONLY_STEPS:]
+        for step, (pair, n) in enumerate(shared_order, ROUTED_ONLY_STEPS):
+            add_shared_and_store(2 * pair, n)
+            add_shared_and_store(2 * pair + 1, n)
+            if 0 <= step - FIRST_MIXED_STEP < len(routed_left):
+                routed_product(*routed_left[step - FIRST_MIXED_STEP])
+                gate_routed(*routed_left[step - FIRST_MIXED_STEP])
+            side_work(step)
+
+        add_shared_and_store(4, last)
+        copy_shared(7, last)
+        add_shared_and_store(5, last)
+        add_shared_and_store(6, last)
+        add_routed_and_store(7, last)

from contextlib import ExitStack

import concourse.mybir as mybir
from concourse.masks import make_identity

M, K, F = 1024, 512, 1536
FLOPS = 2 * M * K * F + 2 * M * M * F + 2 * M * F * F

F32 = mybir.dt.float32
BF16 = mybir.dt.bfloat16
I32 = mybir.dt.int32
U32 = mybir.dt.uint32
U8 = mybir.dt.uint8
FP8X4 = mybir.dt.float8_e4m3fn_x4
FP4X4 = mybir.dt.float4_e2m1fn_x4
ACT = mybir.ActivationFunctionType
ALU = mybir.AluOpType

P = 128
PACK = 4
PASS = P * PACK
QUADRANT = 32
GROUPS = M // PASS
TILES = M // P
CHUNKS = F // PASS
BANKS = 8

VECTOR, SCALAR = "vector", "scalar"
W_COLUMNS_ON_VECTOR = (320, 320, 448)

ROUTED_ONLY_STEPS = 16
FIRST_MIXED_STEP = 18
LAST_TURN_STEP = 5
MIX_START = 4
MIX_TRANSPOSE_LAG, MIX_PAIR_LAG, MIX_QUANTIZE_LAG = 1, 3, 5
INTERLEAVE_ON_VECTOR = {2: (1, 0), 7: (1, 1)}
INTERLEAVE_ON_SCALAR = {18: (0, 2), 19: (1, 2)}
QUANTIZE_H = {1: (0, 0), 2: (0, 1), 3: (1, 0), 8: (1, 1), 20: (0, 2), 21: (1, 2)}


def tile_mixer_expert_pair_s8_kernel(tc, x, w_in, mix, gate, routed_words, routed_scales, out):
    nc = tc.nc
    with ExitStack() as ctx:
        keep = ctx.enter_context(tc.tile_pool(name="keep", bufs=1))
        stage = ctx.enter_context(tc.tile_pool(name="stage", bufs=1))
        psum = ctx.enter_context(tc.psum_pool(name="psum", bufs=1))
        ctx.enter_context(tc.manual_schedule())

        x_rows = x.rearrange("(g p t) k -> g p t k", g=GROUPS, t=PACK)
        out_rows = out.rearrange("(g p t) f -> g t p f", g=GROUPS, t=PACK)
        w_rows = w_in.rearrange("(p j) f -> p j f", j=PACK)

        loaded = {}
        turned = {}
        grouped = {}
        codes = {}
        scales = {}
        hidden = {}
        ordered = {}
        result = {}

        free_banks = list(range(BANKS))
        held = {}

        def take_bank(key):
            index = free_banks[0]
            free_banks.remove(index)
            bank = psum.tile([P, PASS], F32, name="bank%d" % index, tag="bank%d" % index)
            held[key] = (index, bank)
            return bank

        def release_bank(key):
            index, bank = held[key]
            free_banks.append(index)
            return bank

        identity = keep.tile([P, P], F32, name="identity")
        r_scales = keep.tile([P, CHUNKS, F], U8, name="r_scales", align_bytes=64)
        gate_bf16 = keep.tile([P, GROUPS, PACK], BF16, name="gate_bf16")
        gate_f32 = keep.tile([P, TILES], F32, name="gate_f32")
        first_in = keep.tile([P, 1], F32, name="first_in")
        first_out = keep.tile([P, 1], F32, name="first_out")

        nc.vector.memset(first_in[:], 0.0)
        nc.scalar.activation(out=first_out[:], in_=first_in[:], func=ACT.Relu)
        make_identity(nc, identity[:])
        nc.gpsimd.memset(r_scales[:].rearrange("p g n -> p (g n)").bitcast(I32), 0)

        def load_x(pair):
            loaded["x", pair] = keep.tile([P, 2, K], BF16, name="x_rows%d" % pair)
            t = 2 * (pair % 2)
            nc.sync.dma_start(out=loaded["x", pair][:], in_=x_rows[pair // 2, :, t : t + 2, :])

        def load_w(c):
            loaded["w", c] = keep.tile([P, PACK, PASS], BF16, name="w_rows%d" % c)
            nc.sync.dma_start(out=loaded["w", c][:], in_=w_rows[:, :, c * PASS : (c + 1) * PASS])

        def load_gate():
            nc.sync.dma_start(out=gate_bf16[:], in_=gate.rearrange("(g p t) -> p g t", g=GROUPS, t=PACK))
            nc.gpsimd.tensor_copy(out=gate_f32[:], in_=gate_bf16[:].rearrange("p g t -> p (g t)"))

        def load_routed_weight():
            for g in range(CHUNKS):
                loaded["r", g] = keep.tile([P, 2 * F], U8, name="r_words%d" % g, align_bytes=64)
                nc.sync.dma_start(out=loaded["r", g][:].bitcast(I32), in_=routed_words[g].bitcast(I32))
            for q in range(4):
                nc.sync.dma_start(
                    out=r_scales[QUADRANT * q : QUADRANT * q + 4, :, :].bitcast(I32),
                    in_=routed_scales[:, 4 * q : 4 * q + 4, :].rearrange("g r n -> r g n").bitcast(I32),
                )

        def load_mix(group):
            loaded["mix", group] = keep.tile([P, 4, PACK * GROUPS, P], BF16, name="mix_rows%d" % group)
            rows = mix[group * PASS : (group + 1) * PASS, :].rearrange(
                "(b j t) (g q w) -> b q j (t g) w", b=4, t=PACK, g=GROUPS, q=4
            )
            for b in range(4):
                for q in (0, 2, 1, 3):
                    nc.sync.dma_start(
                        out=loaded["mix", group][QUADRANT * q : QUADRANT * (q + 1), b, :, :], in_=rows[b, q]
                    )

        def copy_on(engine, dst, src):
            if engine == VECTOR:
                nc.vector.tensor_copy(out=dst, in_=src)
            else:
                nc.scalar.copy(out=dst, in_=src)

        def new_wide_group(key):
            grouped[key] = stage.tile([P, PASS, PACK], BF16, name="wide", tag="wide", bufs=3, align_bytes=64)

        def interleave(key, src, engine, lo, hi):
            copy_on(
                engine,
                grouped[key][:, lo:hi, :].rearrange("p (c i) t -> p c t i", i=4),
                src[:, :, lo:hi].rearrange("p t (c i) -> p c t i", i=4),
            )

        def interleave_w(c):
            new_wide_group(("w", c))
            interleave(("w", c), loaded["w", c], VECTOR, 0, W_COLUMNS_ON_VECTOR[c])
            interleave(("w", c), loaded["w", c], SCALAR, W_COLUMNS_ON_VECTOR[c], PASS)

        def interleave_h(g, c, engine):
            new_wide_group(("h", g, c))
            interleave(("h", g, c), hidden[g, c], engine, 0, PASS)

        def interleave_h_on_gpsimd(g, c):
            new_wide_group(("h", g, c))
            for lo in range(0, PASS, P):
                nc.gpsimd.tensor_scalar(
                    out=grouped["h", g, c][:, lo : lo + P, :],
                    in0=hidden[g, c][:, :, lo : lo + P].rearrange("p t c -> p c t"),
                    scalar1=1.0,
                    scalar2=0.0,
                    op0=ALU.mult,
                    op1=ALU.add,
                )

        def quantize(key):
            columns = grouped[key].shape[1]
            label = "_".join(str(part) for part in key)
            codes[key] = keep.tile([P, columns], U32, name="codes_" + label, align_bytes=64)
            scales[key] = keep.tile([P, columns], U8, name="scales_" + label, align_bytes=64)
            nc.vector.quantize_mx(
                out=codes[key][:].bitcast(FP8X4),
                scales=scales[key][:],
                in_=grouped[key][:].rearrange("p c t -> p (c t)"),
            )

        def transpose_x(pair):
            bank = take_bank(("x", pair))
            for half in range(2):
                words = loaded["x", pair][:, half, :].bitcast(F32)
                for u in range(2):
                    slot = 2 * half + u
                    nc.tensor.transpose(bank[:, slot * P : (slot + 1) * P], words[:, u : 2 * P : 2], identity[:])

        def transpose_h(pair, c):
            bank = take_bank(("ht", pair, c))
            for half in range(2):
                g, t = divmod(2 * pair + half, PACK)
                words = hidden[g, c][:, t, :].bitcast(F32)
                for u in range(2):
                    slot = 2 * half + u
                    nc.tensor.transpose(bank[:, slot * P : (slot + 1) * P], words[:, u * P : (u + 1) * P], identity[:])

        def order_mix(i):
            group, t = divmod(i, PACK)
            ordered[i] = stage.tile([P, PASS], F32, name="ordered", tag="ordered", bufs=3, align_bytes=64)
            words = loaded["mix", group][:, :, GROUPS * t : GROUPS * (t + 1), :].bitcast(F32)
            nc.vector.tensor_copy(
                out=ordered[i][:].rearrange("p (g u b w) -> p g u b w", g=GROUPS, u=2, b=4),
                in_=words.rearrange("p b g (w u) -> p g u b w", u=2),
            )

        def transpose_mix(i):
            turned["mix", i] = stage.tile([P, PASS], F32, name="blocks", tag="blocks", bufs=4, align_bytes=64)
            nc.vector.transpose(turned["mix", i][:], ordered[i][:])

        def pair_words(key, engine):
            src = turned[key] if key in turned else release_bank(key)
            grouped[key] = stage.tile([P, 2 * P, PACK], BF16, name="paired", tag="paired", bufs=8, align_bytes=64)
            dst = grouped[key][:].rearrange("p c t -> p (c t)").bitcast(F32)
            copy_on(
                engine,
                dst.rearrange("p (half c u) -> p half c u", half=2, u=2),
                src[:].rearrange("p (half u c) -> p half c u", half=2, u=2),
            )

        def hidden_product(i, c):
            tokens = slice(P * (i % 2), P * (i % 2 + 1))
            nc.tensor.matmul_mx(
                out=take_bank(("hidden", i, c))[:],
                lhsT=codes["x", i // 2][:, tokens].bitcast(FP8X4),
                lhsT_scale=scales["x", i // 2][:, tokens],
                rhs=codes["w", c][:].bitcast(FP8X4),
                rhs_scale=scales["w", c][:],
                start=True,
                stop=True,
            )

        def relu_out(i, c, engine):
            g, t = divmod(i, PACK)
            if (g, c) not in hidden:
                hidden[g, c] = keep.tile([P, PACK, PASS], BF16, name="hidden%d_%d" % (g, c), align_bytes=64)
            dst = hidden[g, c][:, t, :].rearrange("p (u m e) -> p u m e", u=2, e=2)
            src = release_bank(("hidden", i, c))[:].rearrange("p (m u e) -> p u m e", u=2, e=2)
            if engine == VECTOR:
                nc.vector.tensor_relu(out=dst, in_=src)
            else:
                nc.scalar.activation(out=dst, in_=src, func=ACT.Relu)

        def routed_product(i, n):
            bank = take_bank(("routed", i, n))
            tokens = slice(P * (i % 2), P * (i % 2 + 1))
            for g in range(CHUNKS):
                nc.tensor.matmul_mx(
                    out=bank[:],
                    lhsT=codes["ht", i // 2, g][:, tokens].bitcast(FP8X4),
                    lhsT_scale=scales["ht", i // 2, g][:, tokens],
                    rhs=loaded["r", g][:, 2 * PASS * n : 2 * PASS * (n + 1)].bitcast(FP4X4),
                    rhs_scale=r_scales[:, g, PASS * n : PASS * (n + 1)],
                    start=(g == 0),
                    stop=(g == CHUNKS - 1),
                )

        def shared_product(i, n):
            bank = take_bank(("shared", i, n))
            for g in range(GROUPS):
                tokens = slice(P * g, P * (g + 1))
                nc.tensor.matmul_mx(
                    out=bank[:],
                    lhsT=codes["mix", i][:, tokens].bitcast(FP8X4),
                    lhsT_scale=scales["mix", i][:, tokens],
                    rhs=codes["h", g, n][:].bitcast(FP8X4),
                    rhs_scale=scales["h", g, n][:],
                    start=(g == 0),
                    stop=(g == GROUPS - 1),
                )

        def gate_routed(i, n):
            result[i, n] = keep.tile([P, PASS], F32, name="result%d_%d" % (i, n))
            nc.scalar.activation(
                out=result[i, n][:],
                in_=release_bank(("routed", i, n))[:],
                func=ACT.Copy,
                scale=gate_f32[:, i : i + 1],
            )

        def store(i, n, lo, hi):
            nc.sync.dma_start(
                out=out_rows[i // PACK, i % PACK, :, n * PASS + lo : n * PASS + hi], in_=result[i, n][:, lo:hi]
            )

        def add_shared_and_store(i, n):
            shared_product(i, n)
            total = result[i, n][:].rearrange("p (m u e) -> p m u e", u=2, e=2)
            nc.vector.tensor_tensor(
                out=total,
                in0=release_bank(("shared", i, n))[:].rearrange("p (u m e) -> p m u e", u=2, e=2),
                in1=total,
                op=ALU.add,
            )
            store(i, n, 0, PASS)

        def copy_shared(i, n):
            shared_product(i, n)
            result[i, n] = keep.tile([P, PASS], F32, name="result%d_%d" % (i, n))
            nc.scalar.copy(
                out=result[i, n][:].rearrange("p (m u e) -> p m u e", u=2, e=2),
                in_=release_bank(("shared", i, n))[:].rearrange("p (u m e) -> p m u e", u=2, e=2),
            )

        def add_routed_and_store(i, n):
            routed_product(i, n)
            bank = release_bank(("routed", i, n))
            for lo in (0, PASS // 2):
                hi = lo + PASS // 2
                nc.vector.scalar_tensor_tensor(
                    out=result[i, n][:, lo:hi],
                    in0=bank[:, lo:hi],
                    scalar=gate_f32[:, i : i + 1],
                    in1=result[i, n][:, lo:hi],
                    op0=ALU.mult,
                    op1=ALU.add,
                )
                store(i, n, lo, hi)

        def turn_h(pieces, engines):
            for pair, c in pieces:
                transpose_h(pair, c)
            for (pair, c), engine in zip(pieces, engines):
                pair_words(("ht", pair, c), engine)

        load_x(0)
        for c in range(CHUNKS):
            load_x(c + 1)
            load_w(c)
        load_gate()
        load_routed_weight()
        for group in range(GROUPS):
            load_mix(group)

        for pair in range(3):
            transpose_x(pair)
        pair_words(("x", 0), VECTOR)
        interleave_w(0)
        pair_words(("x", 1), SCALAR)
        quantize(("x", 0))
        quantize(("w", 0))
        interleave_w(1)
        pair_words(("x", 2), SCALAR)
        quantize(("x", 1))
        quantize(("w", 1))
        quantize(("x", 2))
        hidden_product(0, 0)
        relu_out(0, 0, SCALAR)
        transpose_x(3)
        interleave_w(2)
        pair_words(("x", 3), SCALAR)
        quantize(("x", 3))
        quantize(("w", 2))

        hidden_order = [(1, 0), (0, 1), (1, 1), (2, 0), (3, 0), (2, 1), (3, 1), (4, 0), (5, 0)]
        hidden_order += [(i, 2) for i in range(PACK)]
        hidden_order += [(4, 1), (5, 1), (6, 0), (7, 0), (6, 1), (7, 1)]
        for count, (i, c) in enumerate(hidden_order):
            hidden_product(i, c)
            relu_out(i, c, VECTOR if count >= 2 and count % 2 == 0 else SCALAR)
        interleave_h_on_gpsimd(0, 0)
        interleave_h_on_gpsimd(0, 1)

        pieces = [(pair, c) for pair in range(TILES // 2) for c in range(CHUNKS)]
        turn_h(pieces[:4], (SCALAR, VECTOR, SCALAR, VECTOR))
        for i in range(PACK, TILES):
            hidden_product(i, 2)
        for pair, c in pieces[:CHUNKS]:
            quantize(("ht", pair, c))
        for i in range(PACK, TILES):
            relu_out(i, 2, SCALAR)
        turn_h(pieces[4:8], (VECTOR, SCALAR, VECTOR, SCALAR))

        def side_work(step):
            entry = [MIX_START + 3 * i // 2 for i in range(TILES)]
            if step - MIX_PAIR_LAG in entry:
                pair_words(("mix", entry.index(step - MIX_PAIR_LAG)), SCALAR)
            if step in entry:
                order_mix(entry.index(step))
            if step in INTERLEAVE_ON_SCALAR:
                interleave_h(*INTERLEAVE_ON_SCALAR[step], SCALAR)
            if step - MIX_TRANSPOSE_LAG in entry:
                transpose_mix(entry.index(step - MIX_TRANSPOSE_LAG))
            if step in QUANTIZE_H:
                quantize(("h",) + QUANTIZE_H[step])
            if step - MIX_QUANTIZE_LAG in entry:
                quantize(("mix", entry.index(step - MIX_QUANTIZE_LAG)))

        routed_order = [(i, n) for i in range(PACK) for n in range(CHUNKS)]
        routed_order += [(i, n) for n in range(CHUNKS) for i in range(PACK, TILES)][:-1]
        for step, (i, n) in enumerate(routed_order[:ROUTED_ONLY_STEPS]):
            routed_product(i, n)
            if step == 0:
                for pair, c in pieces[CHUNKS:8]:
                    quantize(("ht", pair, c))
            if step == LAST_TURN_STEP:
                turn_h(pieces[8:], (SCALAR,) * 4)
            if step in INTERLEAVE_ON_VECTOR:
                interleave_h(*INTERLEAVE_ON_VECTOR[step], VECTOR)
            gate_routed(i, n)
            if step == LAST_TURN_STEP + 1:
                for pair, c in pieces[8:]:
                    quantize(("ht", pair, c))
            side_work(step)

        last = CHUNKS - 1
        shared_order = [(pair, n) for pair in range(TILES // 2) for n in range(last)] + [(0, last), (1, last)]
        routed_left = routed_order[ROUTED_ONLY_STEPS:]
        for step, (pair, n) in enumerate(shared_order, ROUTED_ONLY_STEPS):
            add_shared_and_store(2 * pair, n)
            add_shared_and_store(2 * pair + 1, n)
            if 0 <= step - FIRST_MIXED_STEP < len(routed_left):
                routed_product(*routed_left[step - FIRST_MIXED_STEP])
                gate_routed(*routed_left[step - FIRST_MIXED_STEP])
            side_work(step)

        add_shared_and_store(4, last)
        copy_shared(7, last)
        add_shared_and_store(5, last)
        add_shared_and_store(6, last)
        add_routed_and_store(7, last)
